import numpy as np
import ml_dtypes


def mxq(x, axis, fmt="e4m3"):
    dtype, down = {"e4m3": (ml_dtypes.float8_e4m3fn, 7), "e5m2": (ml_dtypes.float8_e5m2, 14)}[fmt]
    v = np.moveaxis(np.asarray(x, np.float32).astype(ml_dtypes.bfloat16).astype(np.float64), axis, -1)
    blocks = v.reshape(v.shape[:-1] + (-1, 32))
    amax = np.abs(blocks).max(-1, keepdims=True)
    byte = np.maximum(np.where(amax > 0, np.frexp(amax)[1] - 1 + 127, 0) - down, 1)
    scale = np.exp2(byte - 127.0)
    codes = (blocks / scale).astype(np.float32).astype(dtype).astype(np.float64)
    return np.moveaxis((codes * scale).reshape(v.shape), -1, axis)


WIDE = False


def mx_kscale(k):
    if not WIDE:
        return np.ones(k)
    levels = np.array([10, -10, 5, -5, 0])
    if k % 512:
        return np.exp2(np.random.permutation(np.resize(levels, k // 32))).repeat(32)
    a = np.empty((k // 512, 16))
    for p in range(k // 512):
        a[p, :8] = np.random.permutation(np.resize(levels, 8))
        for g in range(8):
            far = levels[np.abs(levels - a[p, g]) >= 10]
            a[p, g + 8] = far[np.random.randint(len(far))]
    return np.exp2(a.ravel()).repeat(32)


def f64(x):
    return np.asarray(x).astype(np.float64)


def striped(idx):
    return np.tile(idx.reshape(-1, 16).T, (8, 1)).astype(np.uint16)


def unstriped(offs):
    return offs[:16].T.reshape(-1).astype(np.int64)


def striped8(idx):
    return np.concatenate([x.reshape(-1, 16).T for x in idx]).astype(np.uint16)


def runs(offs, k):
    lists = np.stack([offs[16 * r : 16 * r + 16].T.reshape(-1) for r in range(8)]).astype(np.int64)
    return lists[np.arange(k) % 512 // 64]


def pack_weight(w):
    k, n = w.shape
    w = f64(np.asarray(w, np.float32).astype(ml_dtypes.bfloat16)).reshape(k // 32, 32, n)
    amax = np.abs(w).max(1)
    byte = np.clip(np.where(amax > 0, np.frexp(amax)[1] - 1 + 127 - 7, 1), 1, 254)
    scaled = (w * np.exp2(127.0 - byte)[:, None, :]).reshape(k, n).astype(np.float32)
    words = np.ascontiguousarray(scaled.reshape(k // 512, 128, 4, n).transpose(0, 1, 3, 2)).astype(ml_dtypes.float8_e4m3fn).view(np.uint8)
    return words, np.ascontiguousarray(byte.astype(np.uint8).reshape(k // 512, 16, n))


def unpack_weight(words, scales):
    g, p, n, _ = words.shape
    vals = np.ascontiguousarray(words).view(ml_dtypes.float8_e4m3fn).astype(np.float64) * np.repeat(np.exp2(scales.astype(np.float64) - 127.0), 8, axis=1)[..., None]
    return vals.transpose(0, 1, 3, 2).reshape(g * 512, n)


E2M1 = np.array([0.0, 0.5, 1.0, 1.5, 2.0, 3.0, 4.0, 6.0, -0.0, -0.5, -1.0, -1.5, -2.0, -3.0, -4.0, -6.0])


def pack_fp4(w):
    k, n = w.shape
    w = f64(np.asarray(w, np.float32).astype(ml_dtypes.bfloat16)).reshape(k // 32, 32, n)
    amax = np.abs(w).max(1)
    mant, ex = np.frexp(amax / 6.0)
    byte = np.clip(np.where(amax > 0, np.where(mant > 0.5, ex, ex - 1) + 127, 1), 1, 254)
    scaled = (w * np.exp2(127.0 - byte)[:, None, :]).reshape(k, n).astype(np.float32)
    c = np.ascontiguousarray(scaled.reshape(k // 512, 128, 4, n).transpose(0, 1, 3, 2)).astype(ml_dtypes.float4_e2m1fn).view(np.uint8) & 0xF
    words = (c[..., 0::2] | (c[..., 1::2] << 4)).reshape(k // 512, 128, 2 * n)
    return np.ascontiguousarray(words), np.ascontiguousarray(byte.astype(np.uint8).reshape(k // 512, 16, n))


def unpack_fp4(words, scales):
    g, _, n = scales.shape
    words = np.ascontiguousarray(words).reshape(g, 128, n, 2)
    nib = np.empty((g, 128, n, 4), np.uint8)
    nib[..., 0::2] = words & 0xF
    nib[..., 1::2] = words >> 4
    vals = E2M1[nib] * np.repeat(np.exp2(scales.astype(np.float64) - 127.0), 8, axis=1)[..., None]
    return vals.transpose(0, 1, 3, 2).reshape(g * 512, n)


def planes(y):
    n, m = y.shape
    v = y.astype(np.float32).astype(ml_dtypes.bfloat16).astype(np.float64).reshape(n // 32, 32, m)
    top = np.abs(v).max(1)
    byte = np.clip(np.where(top > 0, np.frexp(top)[1] - 1 + 127 - 7, 1), 1, 254)
    codes = (v * np.exp2(127.0 - byte)[:, None, :]).reshape(n, m).astype(np.float32).astype(ml_dtypes.float8_e4m3fn).view(np.uint8)
    words = codes.reshape(n // 512, 128, 4, m).transpose(0, 1, 3, 2)
    return np.ascontiguousarray(words), np.ascontiguousarray(byte.astype(np.uint8).reshape(n // 512, 16, m))


K, T, S, N, H, U = 512, 2048, 512, 512, 512, 1024


def setup_inputs():
    n = np.random.standard_normal
    s = mx_kscale(K)[:, None]
    u = mx_kscale(H)
    packed_xT = pack_weight(n((K, T)) * s)
    packed_w1 = pack_fp4(n((K, H)) / np.sqrt(K) / s)
    packed_w2 = pack_fp4(n((H, N)) / np.sqrt(2 * H) / u[:, None])
    packed_w3 = pack_fp4(n((H, N)) / np.sqrt(2 * H) / u[:, None])
    return {
        "x_words": packed_xT[0],
        "x_scales": packed_xT[1],
        "w1_words": packed_w1[0],
        "w1_scales": packed_w1[1],
        "gn": (np.random.uniform(0.5, 1.5, (H, 1)) * u[:, None]).astype(np.float32),
        "gm": (np.random.uniform(0.5, 1.5, (H, 1)) * u[:, None]).astype(np.float32),
        "w2_words": packed_w2[0],
        "w2_scales": packed_w2[1],
        "w3_words": packed_w3[0],
        "w3_scales": packed_w3[1],
        "mem": n((N, U)).astype(np.float32),
        "offs": striped(np.random.permutation(T)[:S]),
        "n1": striped8(np.stack([np.random.permutation(S) for _ in range(8)])),
        "n2": striped8(np.stack([np.random.permutation(S) for _ in range(8)])),
        "n3": striped8(np.stack([np.random.permutation(S) for _ in range(8)])),
        "n4": striped8(np.stack([np.random.permutation(S) for _ in range(8)])),
        "n5": striped8(np.stack([np.random.permutation(U)[:S] for _ in range(8)])),
        "n6": striped8(np.stack([np.random.permutation(U) for _ in range(8)])),
    }


def reference(x_words, x_scales, w1_words, w1_scales, gn, gm, w2_words, w2_scales, w3_words, w3_scales, mem, offs, n1, n2, n3, n4, n5, n6):
    xq = unpack_weight(x_words, x_scales)[:, unstriped(offs)]
    y = unpack_fp4(w1_words, w1_scales).T @ xq
    z = f64(gn) * ((y[np.arange(H)[:, None], runs(n1, H)]) / (np.abs(y) + np.abs(y[np.arange(H)[:, None], runs(n2, H)]) + 0.5))
    z2 = f64(gm) * (y[np.arange(H)[:, None], runs(n3, H)] + 0.75 * (y[np.arange(H)[:, None], runs(n4, H)]))
    h = unpack_fp4(w2_words, w2_scales).T @ mxq(z, 0, "e4m3") + unpack_fp4(w3_words, w3_scales).T @ mxq(z2, 0, "e4m3")
    pg = f64(mem).copy()
    pg[np.arange(N)[:, None], runs(n5, N)] = h
    out_0 = pg - (0.5 * (pg[np.arange(N)[:, None], runs(n6, N)]))
    return (out_0,) + planes(out_0)

@@ -1,0 +1,277 @@
+from contextlib import ExitStack
+
+import concourse.mybir as mybir
+
+K, T, S, N, H, U = 512, 2048, 512, 512, 512, 1024
+FLOPS = 2 * K * H * S + 2 * 2 * H * N * S
+
+F32 = mybir.dt.float32
+BF16 = mybir.dt.bfloat16
+I32 = mybir.dt.int32
+U32 = mybir.dt.uint32
+U16 = mybir.dt.uint16
+U8 = mybir.dt.uint8
+FP8X4 = mybir.dt.float8_e4m3fn_x4
+FP4X4 = mybir.dt.float4_e2m1fn_x4
+ACT = mybir.ActivationFunctionType
+ALU = mybir.AluOpType
+
+P = 128
+PACK = 4
+HALF = S // 2
+PASS_N = 128
+OUT_CHUNKS = ((0, 256), (256, 768), (768, 1024))
+
+
+def tile_picked_joinnorm2sumpagem_none_po_kernel(
+    tc, x_words, x_scales, w1_words, w1_scales, gn, gm, w2_words, w2_scales, w3_words, w3_scales, mem,
+    offs, n1, n2, n3, n4, n5, n6, out_0, out_1, out_2,
+):
+    nc = tc.nc
+    with ExitStack() as ctx:
+        lists = ctx.enter_context(tc.tile_pool(name="lists", bufs=1))
+        keep = ctx.enter_context(tc.tile_pool(name="keep", bufs=1))
+        psum = ctx.enter_context(tc.psum_pool(name="psum", bufs=1))
+
+        def load_list(ap, name):
+            t = lists.tile(list(ap.shape), U16, name=name)
+            nc.sync.dma_start(t[:], ap)
+            return t
+
+        def load_scale_rows(dst, src, queue):
+            for q in range(4):
+                queue.dma_start(dst[32 * q : 32 * q + 4, :].bitcast(I32), src[0, 4 * q : 4 * q + 4, :].bitcast(I32))
+
+        def deal_words(raw, name):
+            dealt = keep.tile([P, 2 * H], U8, name=name, align_bytes=64)
+            nc.vector.tensor_copy(
+                dealt[:].bitcast(U16).rearrange("p (t c i) -> p c t i", t=PACK, i=8),
+                raw[:].bitcast(U16).rearrange("p (c i t) -> p c t i", t=PACK, i=8),
+            )
+            return dealt
+
+        def deal_scales(raw, name):
+            dealt = keep.tile([P, H], U8, name=name, align_bytes=64)
+            nc.vector.tensor_copy(
+                dealt[:].rearrange("p (t c i) -> p c t i", t=PACK, i=16),
+                raw.rearrange("p (c i t) -> p c t i", t=PACK, i=16),
+            )
+            return dealt
+
+        def interleave(engine_copy, dst, src):
+            engine_copy(
+                dst[:].rearrange("p (c i t) -> p c t i", t=PACK, i=4),
+                src.rearrange("p t (c i) -> p c t i", i=4),
+            )
+
+        xs_raw = keep.tile([P, T], U8, name="xs_raw", tag="slot1", align_bytes=64)
+        w1s_raw = keep.tile([P, H], U8, name="w1s_raw", tag="slot3", align_bytes=64)
+        w23s_raw = keep.tile([P, 2 * H], U8, name="w23s_raw", align_bytes=64)
+        one = keep.tile([P, 1], F32, name="one")
+        ym = [keep.tile([P, 2 * S], F32, name="ym%d" % t) for t in range(PACK)]
+        nc.vector.memset(xs_raw[:].bitcast(I32), 0)
+        nc.vector.memset(w1s_raw[:].bitcast(I32), 0)
+        nc.vector.memset(w23s_raw[:].bitcast(I32), 0)
+        nc.gpsimd.memset(one[:], 1.0)
+        for t in range(PACK):
+            nc.scalar.activation(ym[t][:, S:], one[:].to_broadcast([P, S]), ACT.Abs_reciprocal_sqrt)
+
+        offs_t = load_list(offs, "offs_t")
+        load_scale_rows(xs_raw, x_scales, nc.sync)
+        w1_raw = keep.tile([P, 2 * H], U8, name="w1_raw", tag="slot2", align_bytes=64)
+        nc.sync.dma_start(w1_raw[:].bitcast(I32), w1_words[0].bitcast(I32))
+        xw_raw = keep.tile([P, T], U32, name="xw_raw", tag="slot0", align_bytes=64)
+        nc.sync.dma_start(xw_raw[:].bitcast(I32), x_words[0].rearrange("p n t -> p (n t)").bitcast(I32))
+        load_scale_rows(w1s_raw, w1_scales, nc.sync)
+        gm_t = keep.tile([P, PACK], F32, name="gm_t", tag="after_gm", align_bytes=64)
+        nc.sync.dma_start(gm_t[:], gm.rearrange("(p t) o -> p (t o)", t=PACK))
+        n4_t = load_list(n4, "n4_t")
+        n3_t = load_list(n3, "n3_t")
+        gn_t = keep.tile([P, PACK], F32, name="gn_t")
+        nc.sync.dma_start(gn_t[:], gn.rearrange("(p t) o -> p (t o)", t=PACK))
+        n2_t = load_list(n2, "n2_t")
+        n1_t = load_list(n1, "n1_t")
+
+        w3_raw = keep.tile([P, 2 * H], U8, name="w3_raw", align_bytes=64)
+        nc.sync.dma_start(w3_raw[:].bitcast(I32), w3_words[0].bitcast(I32))
+        w2_raw = keep.tile([P, 2 * H], U8, name="w2_raw", align_bytes=64)
+        nc.sync.dma_start(w2_raw[:].bitcast(I32), w2_words[0].bitcast(I32))
+        load_scale_rows(w23s_raw[:, :H], w2_scales, nc.sync)
+        load_scale_rows(w23s_raw[:, H:], w3_scales, nc.sync)
+        n5_t = load_list(n5, "n5_t")
+        n6_t = load_list(n6, "n6_t")
+
+        xs = keep.tile([P, S], U8, name="xs", align_bytes=64)
+        nc.vector.tensor_copy(xs[:], xs_raw[:].indirect(offs_t[:]))
+        w1 = deal_words(w1_raw, "w1")
+        xw = keep.tile([P, S], U32, name="xw", align_bytes=64)
+        nc.vector.tensor_copy(xw[:], xw_raw[:].indirect(offs_t[:]))
+        w1s = deal_scales(w1s_raw[:], "w1s")
+
+        pg = []
+        mem_rows = mem.rearrange("(p t) w -> p t w", t=PACK)
+        for t in range(PACK):
+            page = keep.tile([P, U], F32, name="pg%d" % t, tag="slot%d" % t, align_bytes=64)
+            nc.sync.dma_start(page[:], mem_rows[:, t, :])
+            pg.append(page)
+
+        y_ps = [psum.tile([P, S], F32, name="y_ps%d" % t) for t in range(PACK)]
+        for t in range(PACK):
+            nc.tensor.matmul_mx(
+                y_ps[t][:],
+                lhsT=w1[:, 2 * P * t : 2 * P * (t + 1)].bitcast(FP4X4),
+                lhsT_scale=w1s[:, P * t : P * (t + 1)],
+                rhs=xw[:].bitcast(FP8X4),
+                rhs_scale=xs[:],
+                start=True,
+                stop=True,
+            )
+
+        ya = [keep.tile([P, 2 * S], F32, name="ya%d" % t) for t in range(PACK)]
+        ya2 = [keep.tile([P, S], F32, name="yb%d" % t) for t in range(PACK)]
+        yn = [keep.tile([P, S], F32, name="yn%d" % t) for t in range(PACK)]
+        for t in range(PACK):
+            nc.scalar.activation(ym[t][:, :S], y_ps[t][:], ACT.Copy, scale=gm_t[:, t : t + 1])
+        for t in range(PACK):
+            nc.scalar.activation(ya[t][:, :S], y_ps[t][:], ACT.Abs)
+            nc.scalar.activation(ya2[t][:], y_ps[t][:], ACT.Abs)
+        for t in range(PACK):
+            nc.scalar.activation(yn[t][:], y_ps[t][:], ACT.Copy, scale=gn_t[:, t : t + 1])
+
+        w3 = deal_words(w3_raw, "w3")
+        w2 = deal_words(w2_raw, "w2")
+        w2s = deal_scales(w23s_raw[:, :H], "w2s")
+        w3s = deal_scales(w23s_raw[:, H:], "w3s")
+
+        halves = [slice(0, HALF), slice(HALF, S)]
+        list_halves = [slice(0, HALF // 16), slice(HALF // 16, S // 16)]
+
+        def tile(shape, dtype, name, tag=None):
+            return keep.tile(shape, dtype, name=name, tag=tag or name, align_bytes=64)
+
+        def pair_sum(dst, a, t):
+            nc.vector.tensor_tensor(
+                dst[:, t, :], ym[t][:].indirect(n3_t[:, list_halves[a]]), ya[t][:, S + a * HALF : S + (a + 1) * HALF], ALU.add
+            )
+
+        def invert(t, a, tag=None):
+            root = tile([P, HALF], F32, "root%d_%d" % (a, t))
+            nc.scalar.activation(root[:], den[t][:, halves[a]], ACT.Abs_reciprocal_sqrt, bias=0.5)
+            inv = tile([P, HALF], F32, "inv%d_%d" % (a, t), tag)
+            nc.scalar.activation(inv[:], root[:], ACT.Square)
+            return inv
+
+        def numerator(dst, a, t, inv):
+            nc.vector.tensor_tensor(dst[:, t, :], yn[t][:].indirect(n1_t[:, list_halves[a]]), inv[:], ALU.mult)
+
+        def round_values(values, name, tag=None):
+            rounded = tile([P, PACK * HALF], BF16, name, tag)
+            interleave(nc.scalar.copy, rounded, values[:])
+            return rounded
+
+        def quantise(rounded, name):
+            codes = tile([P, HALF], U32, name + "_codes")
+            scales = tile([P, HALF], U8, name + "_scales")
+            nc.vector.quantize_mx(codes[:].bitcast(FP8X4), scales[:], rounded[:])
+            return codes, scales
+
+        h_ps = [psum.tile([P, S], F32, name="h_ps%d" % t) for t in range(PACK)]
+
+        def second_product(a, z2q, zq):
+            for t in range(PACK):
+                for c in range(0, HALF, PASS_N):
+                    cols = slice(c, c + PASS_N)
+                    dst = h_ps[t][:, a * HALF + c : a * HALF + c + PASS_N]
+                    for first, w, ws, (codes, scales) in ((True, w3, w3s, z2q), (False, w2, w2s, zq)):
+                        nc.tensor.matmul_mx(
+                            dst,
+                            lhsT=w[:, 2 * P * t : 2 * P * (t + 1)].bitcast(FP4X4),
+                            lhsT_scale=ws[:, P * t : P * (t + 1)],
+                            rhs=codes[:, cols].bitcast(FP8X4),
+                            rhs_scale=scales[:, cols],
+                            start=first,
+                            stop=not first,
+                        )
+
+        def fetch_h(a, t, tag=None):
+            h = tile([P, HALF], F32, "h%d_%d" % (a, t), tag)
+            nc.scalar.copy(h[:], h_ps[t][:, halves[a]])
+            return h
+
+        def scatter(a, t, h):
+            nc.vector.tensor_copy(pg[t][:].indirect(n5_t[:, list_halves[a]]), h[:])
+
+        z2f_a = tile([P, PACK, HALF], F32, "z2f_a", "after_gm")
+        for t in range(PACK):
+            nc.vector.tensor_scalar(ya[t][:, S:], ym[t][:].indirect(n4_t[:]), 0.75, 0.0, ALU.mult, ALU.add)
+        for t in range(PACK):
+            pair_sum(z2f_a, 0, t)
+
+        den = [tile([P, S], F32, "den%d" % t) for t in range(PACK)]
+        inv_a = []
+        for t in range(PACK):
+            nc.vector.tensor_tensor(den[t][:], ya[t][:].indirect(n2_t[:]), ya2[t][:], ALU.add)
+            inv_a.append(invert(t, 0, "after_zf_a" if t == PACK - 1 else None))
+            if t == 0:
+                z2b_a = round_values(z2f_a, "z2b_a")
+        z2q_a = quantise(z2b_a, "z2q_a")
+        zf_a = tile([P, PACK, HALF], F32, "zf_a")
+        for t in range(PACK):
+            numerator(zf_a, 0, t, inv_a[t])
+        inv_b = [invert(t, 1) for t in range(PACK)]
+        zb_a = round_values(zf_a, "zb_a", "chain")
+        z2f_b = tile([P, PACK, HALF], F32, "z2f_b", "after_zf_a")
+        for t in range(PACK):
+            pair_sum(z2f_b, 1, t)
+        zq_a = quantise(zb_a, "zq_a")
+        zf_b = tile([P, PACK, HALF], F32, "zf_b", "chain")
+        for t in range(PACK):
+            numerator(zf_b, 1, t, inv_b[t])
+        second_product(0, z2q_a, zq_a)
+        for t in range(2):
+            scatter(0, t, fetch_h(0, t))
+        zb_b = round_values(zf_b, "zb_b", "after_zq_b")
+        z2b_b = round_values(z2f_b, "z2b_b", "chain")
+        zq_b = quantise(zb_b, "zq_b")
+        z2q_b = quantise(z2b_b, "z2q_b")
+        scatter(0, 2, fetch_h(0, 2, "after_zq_b"))
+        scatter(0, 3, fetch_h(0, 3, "chain"))
+        second_product(1, z2q_b, zq_b)
+        neg_half = [keep.tile([P, U], F32, name="nh%d" % t) for t in range(PACK)]
+        for t in range(PACK):
+            scatter(1, t, fetch_h(1, t))
+            nc.scalar.activation(neg_half[t][:], pg[t][:], ACT.Copy, scale=-0.5)
+
+        out_rows = out_0.rearrange("(p t) w -> p t w", t=PACK)
+        words_out = out_1[0].rearrange("p n t -> p (n t)").bitcast(I32)
+        out_scales = keep.tile([P, U], U8, name="out_scales", align_bytes=64)
+        pending = []
+
+        def finish(k, lo, hi, res):
+            last = k == len(OUT_CHUNKS) - 1
+            rounded = keep.tile([P, PACK * (hi - lo)], BF16, name="rounded%d" % k, align_bytes=64)
+            interleave(nc.vector.tensor_copy if last else nc.scalar.copy, rounded, res[:])
+            return rounded
+
+        def quantise_out(k, lo, hi, rounded):
+            codes = keep.tile([P, hi - lo], U32, name="codes%d" % k, align_bytes=64)
+            nc.vector.quantize_mx(codes[:].bitcast(FP8X4), out_scales[:, lo:hi], rounded[:])
+            nc.sync.dma_start(words_out[:, lo:hi], codes[:].bitcast(I32))
+
+        for k, (lo, hi) in enumerate(OUT_CHUNKS):
+            res = keep.tile([P, PACK, hi - lo], F32, name="res%d" % k)
+            for t in range(PACK):
+                nc.vector.tensor_tensor(
+                    res[:, t, :], neg_half[t][:].indirect(n6_t[:, lo // 16 : hi // 16]), pg[t][:, lo:hi], ALU.add
+                )
+                if k == 0:
+                    nc.sync.dma_start(out_rows[:, t, lo:hi], res[:, t, :])
+                elif t % 2 == 1:
+                    nc.sync.dma_start(out_rows[:, t - 1 : t + 1, lo:hi], res[:, t - 1 : t + 1, :])
+                if t == PACK - 1 and pending:
+                    quantise_out(*pending.pop())
+            pending.append((k, lo, hi, finish(k, lo, hi, res)))
+        quantise_out(*pending.pop())
+        for q in range(4):
+            queue = nc.sync if q % 2 == 0 else nc.scalar
+            queue.dma_start(out_2[0, 4 * q : 4 * q + 4, :].bitcast(I32), out_scales[32 * q : 32 * q + 4, :].bitcast(I32))

@@ -20,7 +20,8 @@ P = 128
 PACK = 4
 HALF = S // 2
 PASS_N = 128
-OUT_CHUNKS = ((0, 256), (256, 768), (768, 1024))
+OUT_CHUNK = 256
+LAST_SPLIT = 160
 
 
 def tile_picked_joinnorm2sumpagem_none_po_kernel(
@@ -38,9 +39,10 @@ def tile_picked_joinnorm2sumpagem_none_po_kernel(
             nc.sync.dma_start(t[:], ap)
             return t
 
-        def load_scale_rows(dst, src, queue):
+        def load_scale_rows(dst, src, queue, first=0):
             for q in range(4):
-                queue.dma_start(dst[32 * q : 32 * q + 4, :].bitcast(I32), src[0, 4 * q : 4 * q + 4, :].bitcast(I32))
+                row = 32 * q + first
+                queue.dma_start(dst[row : row + 4, :].bitcast(I32), src[0, 4 * q : 4 * q + 4, :].bitcast(I32))
 
         def deal_words(raw, name):
             dealt = keep.tile([P, 2 * H], U8, name=name, align_bytes=64)
@@ -66,23 +68,31 @@ def tile_picked_joinnorm2sumpagem_none_po_kernel(
 
         xs_raw = keep.tile([P, T], U8, name="xs_raw", tag="slot1", align_bytes=64)
         w1s_raw = keep.tile([P, H], U8, name="w1s_raw", tag="slot3", align_bytes=64)
-        w23s_raw = keep.tile([P, 2 * H], U8, name="w23s_raw", align_bytes=64)
-        one = keep.tile([P, 1], F32, name="one")
+        w23s_raw = keep.tile([P, H], U8, name="w23s_raw", align_bytes=64)
+        w3s = keep.tile([P, H], U8, name="w3s", align_bytes=64)
+        one = keep.tile([P, 1], F32, name="one", tag="after_zq_b", align_bytes=64)
+        one_b = keep.tile([P, 1], F32, name="one_b", tag="after_neg_half", align_bytes=64)
         ym = [keep.tile([P, 2 * S], F32, name="ym%d" % t) for t in range(PACK)]
         nc.vector.memset(xs_raw[:].bitcast(I32), 0)
         nc.vector.memset(w1s_raw[:].bitcast(I32), 0)
         nc.vector.memset(w23s_raw[:].bitcast(I32), 0)
+        nc.vector.memset(w3s[:].bitcast(I32), 0)
         nc.gpsimd.memset(one[:], 1.0)
+        nc.gpsimd.memset(one_b[:], 1.0)
         for t in range(PACK):
             nc.scalar.activation(ym[t][:, S:], one[:].to_broadcast([P, S]), ACT.Abs_reciprocal_sqrt)
 
         offs_t = load_list(offs, "offs_t")
-        load_scale_rows(xs_raw, x_scales, nc.sync)
         w1_raw = keep.tile([P, 2 * H], U8, name="w1_raw", tag="slot2", align_bytes=64)
         nc.sync.dma_start(w1_raw[:].bitcast(I32), w1_words[0].bitcast(I32))
+        w3_raw = keep.tile([P, 2 * H], U8, name="w3_raw", align_bytes=64)
+        nc.sync.dma_start(w3_raw[:].bitcast(I32), w3_words[0].bitcast(I32))
+        load_scale_rows(xs_raw, x_scales, nc.sync)
         xw_raw = keep.tile([P, T], U32, name="xw_raw", tag="slot0", align_bytes=64)
         nc.sync.dma_start(xw_raw[:].bitcast(I32), x_words[0].rearrange("p n t -> p (n t)").bitcast(I32))
         load_scale_rows(w1s_raw, w1_scales, nc.sync)
+        w2_raw = keep.tile([P, 2 * H], U8, name="w2_raw", align_bytes=64)
+        nc.sync.dma_start(w2_raw[:].bitcast(I32), w2_words[0].bitcast(I32))
         gm_t = keep.tile([P, PACK], F32, name="gm_t", tag="after_gm", align_bytes=64)
         nc.sync.dma_start(gm_t[:], gm.rearrange("(p t) o -> p (t o)", t=PACK))
         n4_t = load_list(n4, "n4_t")
@@ -92,21 +102,24 @@ def tile_picked_joinnorm2sumpagem_none_po_kernel(
         n2_t = load_list(n2, "n2_t")
         n1_t = load_list(n1, "n1_t")
 
-        w3_raw = keep.tile([P, 2 * H], U8, name="w3_raw", align_bytes=64)
-        nc.sync.dma_start(w3_raw[:].bitcast(I32), w3_words[0].bitcast(I32))
-        w2_raw = keep.tile([P, 2 * H], U8, name="w2_raw", align_bytes=64)
-        nc.sync.dma_start(w2_raw[:].bitcast(I32), w2_words[0].bitcast(I32))
-        load_scale_rows(w23s_raw[:, :H], w2_scales, nc.sync)
-        load_scale_rows(w23s_raw[:, H:], w3_scales, nc.sync)
+        load_scale_rows(w23s_raw, w2_scales, nc.sync)
+        load_scale_rows(w23s_raw, w3_scales, nc.sync, 4)
         n5_t = load_list(n5, "n5_t")
         n6_t = load_list(n6, "n6_t")
 
+        w1 = deal_words(w1_raw, "w1")
+        w3 = deal_words(w3_raw, "w3")
         xs = keep.tile([P, S], U8, name="xs", align_bytes=64)
         nc.vector.tensor_copy(xs[:], xs_raw[:].indirect(offs_t[:]))
-        w1 = deal_words(w1_raw, "w1")
         xw = keep.tile([P, S], U32, name="xw", align_bytes=64)
         nc.vector.tensor_copy(xw[:], xw_raw[:].indirect(offs_t[:]))
-        w1s = deal_scales(w1s_raw[:], "w1s")
+        w1s_first = keep.tile([P, P], U8, name="w1s_first", align_bytes=64)
+        nc.vector.tensor_copy(w1s_first[:], w1s_raw[:, 0:H:PACK])
+        w1s_rest = keep.tile([P, H - P], U8, name="w1s_rest", align_bytes=64)
+        nc.vector.tensor_copy(
+            w1s_rest[:].rearrange("p (t c i) -> p c t i", t=PACK - 1, i=16),
+            w1s_raw[:].rearrange("p (c i t) -> p c t i", t=PACK, i=16)[:, :, 1:, :],
+        )
 
         pg = []
         mem_rows = mem.rearrange("(p t) w -> p t w", t=PACK)
@@ -120,7 +133,7 @@ def tile_picked_joinnorm2sumpagem_none_po_kernel(
             nc.tensor.matmul_mx(
                 y_ps[t][:],
                 lhsT=w1[:, 2 * P * t : 2 * P * (t + 1)].bitcast(FP4X4),
-                lhsT_scale=w1s[:, P * t : P * (t + 1)],
+                lhsT_scale=w1s_rest[:, P * (t - 1) : P * t] if t else w1s_first[:],
                 rhs=xw[:].bitcast(FP8X4),
                 rhs_scale=xs[:],
                 start=True,
@@ -138,10 +151,10 @@ def tile_picked_joinnorm2sumpagem_none_po_kernel(
         for t in range(PACK):
             nc.scalar.activation(yn[t][:], y_ps[t][:], ACT.Copy, scale=gn_t[:, t : t + 1])
 
-        w3 = deal_words(w3_raw, "w3")
         w2 = deal_words(w2_raw, "w2")
-        w2s = deal_scales(w23s_raw[:, :H], "w2s")
-        w3s = deal_scales(w23s_raw[:, H:], "w3s")
+        w2s = deal_scales(w23s_raw[:], "w2s")
+        for q in range(4):
+            nc.sync.dma_start(w3s[32 * q : 32 * q + 4, :].bitcast(I32), w2s[32 * q + 4 : 32 * q + 8, :].bitcast(I32))
 
         halves = [slice(0, HALF), slice(HALF, S)]
         list_halves = [slice(0, HALF // 16), slice(HALF // 16, S // 16)]
@@ -193,9 +206,9 @@ def tile_picked_joinnorm2sumpagem_none_po_kernel(
                             stop=not first,
                         )
 
-        def fetch_h(a, t, tag=None):
+        def fetch_h(a, t, scale=1.0, tag=None):
             h = tile([P, HALF], F32, "h%d_%d" % (a, t), tag)
-            nc.scalar.copy(h[:], h_ps[t][:, halves[a]])
+            nc.scalar.activation(h[:], h_ps[t][:, halves[a]], ACT.Copy, scale=scale)
             return h
 
         def scatter(a, t, h):
@@ -229,49 +242,53 @@ def tile_picked_joinnorm2sumpagem_none_po_kernel(
             numerator(zf_b, 1, t, inv_b[t])
         second_product(0, z2q_a, zq_a)
         for t in range(2):
-            scatter(0, t, fetch_h(0, t))
+            scatter(0, t, fetch_h(0, t, one[:]))
         zb_b = round_values(zf_b, "zb_b", "after_zq_b")
         z2b_b = round_values(z2f_b, "z2b_b", "chain")
         zq_b = quantise(zb_b, "zq_b")
         z2q_b = quantise(z2b_b, "z2q_b")
-        scatter(0, 2, fetch_h(0, 2, "after_zq_b"))
-        scatter(0, 3, fetch_h(0, 3, "chain"))
+        scatter(0, 2, fetch_h(0, 2, tag="after_zq_b"))
+        scatter(0, 3, fetch_h(0, 3, tag="chain"))
         second_product(1, z2q_b, zq_b)
+        h_b = [fetch_h(1, t, one_b[:]) for t in range(PACK)]
+        minus_half = tile([P, 1], F32, "minus_half", "after_neg_half")
+        nc.gpsimd.memset(minus_half[:], -0.5)
         neg_half = [keep.tile([P, U], F32, name="nh%d" % t) for t in range(PACK)]
         for t in range(PACK):
-            scatter(1, t, fetch_h(1, t))
-            nc.scalar.activation(neg_half[t][:], pg[t][:], ACT.Copy, scale=-0.5)
+            scatter(1, t, h_b[t])
+            nc.scalar.activation(neg_half[t][:], pg[t][:], ACT.Copy, scale=minus_half[:])
 
         out_rows = out_0.rearrange("(p t) w -> p t w", t=PACK)
         words_out = out_1[0].rearrange("p n t -> p (n t)").bitcast(I32)
         out_scales = keep.tile([P, U], U8, name="out_scales", align_bytes=64)
-        pending = []
 
-        def finish(k, lo, hi, res):
-            last = k == len(OUT_CHUNKS) - 1
-            rounded = keep.tile([P, PACK * (hi - lo)], BF16, name="rounded%d" % k, align_bytes=64)
-            interleave(nc.vector.tensor_copy if last else nc.scalar.copy, rounded, res[:])
-            return rounded
+        def quantise_out(k, rounded):
+            cols = slice(k * OUT_CHUNK, (k + 1) * OUT_CHUNK)
+            codes = tile([P, OUT_CHUNK], U32, "codes%d" % k)
+            nc.vector.quantize_mx(codes[:].bitcast(FP8X4), out_scales[:, cols], rounded[:])
+            nc.sync.dma_start(words_out[:, cols], codes[:].bitcast(I32))
 
-        def quantise_out(k, lo, hi, rounded):
-            codes = keep.tile([P, hi - lo], U32, name="codes%d" % k, align_bytes=64)
-            nc.vector.quantize_mx(codes[:].bitcast(FP8X4), out_scales[:, lo:hi], rounded[:])
-            nc.sync.dma_start(words_out[:, lo:hi], codes[:].bitcast(I32))
-
-        for k, (lo, hi) in enumerate(OUT_CHUNKS):
-            res = keep.tile([P, PACK, hi - lo], F32, name="res%d" % k)
+        chunks = U // OUT_CHUNK
+        rounded = []
+        for k in range(chunks):
+            cols = slice(k * OUT_CHUNK, (k + 1) * OUT_CHUNK)
+            if k >= 2:
+                quantise_out(k - 2, rounded[k - 2])
+            res = tile([P, PACK, OUT_CHUNK], F32, "res%d" % k, "out_chain%d" % (k - 2) if k >= 2 else ("after_neg_half" if k else None))
             for t in range(PACK):
                 nc.vector.tensor_tensor(
-                    res[:, t, :], neg_half[t][:].indirect(n6_t[:, lo // 16 : hi // 16]), pg[t][:, lo:hi], ALU.add
+                    res[:, t, :], neg_half[t][:].indirect(n6_t[:, cols.start // 16 : cols.stop // 16]), pg[t][:, cols], ALU.add
                 )
-                if k == 0:
-                    nc.sync.dma_start(out_rows[:, t, lo:hi], res[:, t, :])
-                elif t % 2 == 1:
-                    nc.sync.dma_start(out_rows[:, t - 1 : t + 1, lo:hi], res[:, t - 1 : t + 1, :])
-                if t == PACK - 1 and pending:
-                    quantise_out(*pending.pop())
-            pending.append((k, lo, hi, finish(k, lo, hi, res)))
-        quantise_out(*pending.pop())
+                if t % 2 == 1:
+                    nc.sync.dma_start(out_rows[:, t - 1 : t + 1, cols], res[:, t - 1 : t + 1, :])
+            rounded.append(tile([P, PACK * OUT_CHUNK], BF16, "rounded%d" % k, "out_chain%d" % k if k < 2 else None))
+            if k < chunks - 1:
+                interleave(nc.scalar.copy, rounded[k], res[:])
+            else:
+                interleave(nc.vector.tensor_copy, rounded[k][:, : PACK * LAST_SPLIT], res[:, :, :LAST_SPLIT])
+                interleave(nc.scalar.copy, rounded[k][:, PACK * LAST_SPLIT :], res[:, :, LAST_SPLIT:])
+        quantise_out(chunks - 2, rounded[chunks - 2])
+        quantise_out(chunks - 1, rounded[chunks - 1])
         for q in range(4):
             queue = nc.sync if q % 2 == 0 else nc.scalar
             queue.dma_start(out_2[0, 4 * q : 4 * q + 4, :].bitcast(I32), out_scales[32 * q : 32 * q + 4, :].bitcast(I32))

@@ -79,6 +79,8 @@ def tile_picked_joinnorm2sumpagem_none_po_kernel(
         nc.vector.memset(w3s[:].bitcast(I32), 0)
         nc.gpsimd.memset(one[:], 1.0)
         nc.gpsimd.memset(one_b[:], 1.0)
+        one_c = keep.tile([P, 1], F32, name="one_c")
+        nc.gpsimd.memset(one_c[:], 1.0)
         for t in range(PACK):
             nc.scalar.activation(ym[t][:, S:], one[:].to_broadcast([P, S]), ACT.Abs_reciprocal_sqrt)
 
@@ -252,7 +254,7 @@ def tile_picked_joinnorm2sumpagem_none_po_kernel(
         second_product(1, z2q_b, zq_b)
         h_b = [fetch_h(1, t, one_b[:]) for t in range(PACK)]
         minus_half = tile([P, 1], F32, "minus_half", "after_neg_half")
-        nc.gpsimd.memset(minus_half[:], -0.5)
+        nc.scalar.activation(minus_half[:], one_c[:], ACT.Copy, scale=-0.5)
         neg_half = [keep.tile([P, U], F32, name="nh%d" % t) for t in range(PACK)]
         for t in range(PACK):
             scatter(1, t, h_b[t])

@@ -21,7 +21,7 @@ PACK = 4
 HALF = S // 2
 PASS_N = 128
 OUT_CHUNK = 256
-LAST_SPLIT = 160
+LAST_SPLIT = 176
 
 
 def tile_picked_joinnorm2sumpagem_none_po_kernel(
@@ -62,8 +62,8 @@ def tile_picked_joinnorm2sumpagem_none_po_kernel(
 
         def interleave(engine_copy, dst, src):
             engine_copy(
-                dst[:].rearrange("p (c i t) -> p c t i", t=PACK, i=4),
-                src.rearrange("p t (c i) -> p c t i", i=4),
+                dst[:].rearrange("p (c t) -> p c t", t=PACK),
+                src.rearrange("p t c -> p c t"),
             )
 
         xs_raw = keep.tile([P, T], U8, name="xs_raw", tag="slot1", align_bytes=64)
@@ -208,13 +208,12 @@ def tile_picked_joinnorm2sumpagem_none_po_kernel(
                             stop=not first,
                         )
 
-        def fetch_h(a, t, scale=1.0, tag=None):
-            h = tile([P, HALF], F32, "h%d_%d" % (a, t), tag)
-            nc.scalar.activation(h[:], h_ps[t][:, halves[a]], ACT.Copy, scale=scale)
+        def fetch_h(h, a, t, scale=1.0):
+            nc.scalar.activation(h, h_ps[t][:, halves[a]], ACT.Copy, scale=scale)
             return h
 
         def scatter(a, t, h):
-            nc.vector.tensor_copy(pg[t][:].indirect(n5_t[:, list_halves[a]]), h[:])
+            nc.vector.tensor_copy(pg[t][:].indirect(n5_t[:, list_halves[a]]), h)
 
         z2f_a = tile([P, PACK, HALF], F32, "z2f_a", "after_gm")
         for t in range(PACK):
@@ -238,21 +237,22 @@ def tile_picked_joinnorm2sumpagem_none_po_kernel(
         z2f_b = tile([P, PACK, HALF], F32, "z2f_b", "after_zf_a")
         for t in range(PACK):
             pair_sum(z2f_b, 1, t)
+        z2b_b = round_values(z2f_b, "z2b_b")
         zq_a = quantise(zb_a, "zq_a")
         zf_b = tile([P, PACK, HALF], F32, "zf_b", "chain")
         for t in range(PACK):
             numerator(zf_b, 1, t, inv_b[t])
+        z2q_b = quantise(z2b_b, "z2q_b")
         second_product(0, z2q_a, zq_a)
         for t in range(2):
-            scatter(0, t, fetch_h(0, t, one[:]))
+            scatter(0, t, fetch_h(tile([P, HALF], F32, "h_a%d" % t)[:], 0, t, one[:]))
         zb_b = round_values(zf_b, "zb_b", "after_zq_b")
-        z2b_b = round_values(z2f_b, "z2b_b", "chain")
         zq_b = quantise(zb_b, "zq_b")
-        z2q_b = quantise(z2b_b, "z2q_b")
-        scatter(0, 2, fetch_h(0, 2, tag="after_zq_b"))
-        scatter(0, 3, fetch_h(0, 3, tag="chain"))
+        h_late = tile([P, 2, HALF], F32, "h_late", "chain")
+        for t in range(2, PACK):
+            scatter(0, t, fetch_h(h_late[:, t - 2, :], 0, t))
         second_product(1, z2q_b, zq_b)
-        h_b = [fetch_h(1, t, one_b[:]) for t in range(PACK)]
+        h_b = [fetch_h(tile([P, HALF], F32, "h_b%d" % t)[:], 1, t, one_b[:]) for t in range(PACK)]
         minus_half = tile([P, 1], F32, "minus_half", "after_neg_half")
         nc.scalar.activation(minus_half[:], one_c[:], ACT.Copy, scale=-0.5)
         neg_half = [keep.tile([P, U], F32, name="nh%d" % t) for t in range(PACK)]

from contextlib import ExitStack

import concourse.mybir as mybir

K, T, S, N, H, U = 512, 2048, 512, 512, 512, 1024
FLOPS = 2 * K * H * S + 2 * 2 * H * N * S

F32 = mybir.dt.float32
BF16 = mybir.dt.bfloat16
I32 = mybir.dt.int32
U32 = mybir.dt.uint32
U16 = mybir.dt.uint16
U8 = mybir.dt.uint8
FP8X4 = mybir.dt.float8_e4m3fn_x4
FP4X4 = mybir.dt.float4_e2m1fn_x4
ACT = mybir.ActivationFunctionType
ALU = mybir.AluOpType

P = 128
PACK = 4
HALF = S // 2
PASS_N = 128
OUT_CHUNK = 256
LAST_SPLIT = 176


def tile_picked_joinnorm2sumpagem_none_po_kernel(
    tc, x_words, x_scales, w1_words, w1_scales, gn, gm, w2_words, w2_scales, w3_words, w3_scales, mem,
    offs, n1, n2, n3, n4, n5, n6, out_0, out_1, out_2,
):
    nc = tc.nc
    with ExitStack() as ctx:
        lists = ctx.enter_context(tc.tile_pool(name="lists", bufs=1))
        keep = ctx.enter_context(tc.tile_pool(name="keep", bufs=1))
        psum = ctx.enter_context(tc.psum_pool(name="psum", bufs=1))

        def load_list(ap, name):
            t = lists.tile(list(ap.shape), U16, name=name)
            nc.sync.dma_start(t[:], ap)
            return t

        def load_scale_rows(dst, src, queue, first=0):
            for q in range(4):
                row = 32 * q + first
                queue.dma_start(dst[row : row + 4, :].bitcast(I32), src[0, 4 * q : 4 * q + 4, :].bitcast(I32))

        def deal_words(raw, name):
            dealt = keep.tile([P, 2 * H], U8, name=name, align_bytes=64)
            nc.vector.tensor_copy(
                dealt[:].bitcast(U16).rearrange("p (t c i) -> p c t i", t=PACK, i=8),
                raw[:].bitcast(U16).rearrange("p (c i t) -> p c t i", t=PACK, i=8),
            )
            return dealt

        def deal_scales(raw, name):
            dealt = keep.tile([P, H], U8, name=name, align_bytes=64)
            nc.vector.tensor_copy(
                dealt[:].rearrange("p (t c i) -> p c t i", t=PACK, i=16),
                raw.rearrange("p (c i t) -> p c t i", t=PACK, i=16),
            )
            return dealt

        def interleave(engine_copy, dst, src):
            engine_copy(
                dst[:].rearrange("p (c t) -> p c t", t=PACK),
                src.rearrange("p t c -> p c t"),
            )

        xs_raw = keep.tile([P, T], U8, name="xs_raw", tag="slot1", align_bytes=64)
        w1s_raw = keep.tile([P, H], U8, name="w1s_raw", tag="slot3", align_bytes=64)
        w23s_raw = keep.tile([P, H], U8, name="w23s_raw", align_bytes=64)
        w3s = keep.tile([P, H], U8, name="w3s", align_bytes=64)
        one = keep.tile([P, 1], F32, name="one", tag="after_zq_b", align_bytes=64)
        one_b = keep.tile([P, 1], F32, name="one_b", tag="after_neg_half", align_bytes=64)
        ym = [keep.tile([P, 2 * S], F32, name="ym%d" % t) for t in range(PACK)]
        nc.vector.memset(xs_raw[:].bitcast(I32), 0)
        nc.vector.memset(w1s_raw[:].bitcast(I32), 0)
        nc.vector.memset(w23s_raw[:].bitcast(I32), 0)
        nc.vector.memset(w3s[:].bitcast(I32), 0)
        nc.gpsimd.memset(one[:], 1.0)
        nc.gpsimd.memset(one_b[:], 1.0)
        one_c = keep.tile([P, 1], F32, name="one_c")
        nc.gpsimd.memset(one_c[:], 1.0)
        for t in range(PACK):
            nc.scalar.activation(ym[t][:, S:], one[:].to_broadcast([P, S]), ACT.Abs_reciprocal_sqrt)

        offs_t = load_list(offs, "offs_t")
        w1_raw = keep.tile([P, 2 * H], U8, name="w1_raw", tag="slot2", align_bytes=64)
        nc.sync.dma_start(w1_raw[:].bitcast(I32), w1_words[0].bitcast(I32))
        w3_raw = keep.tile([P, 2 * H], U8, name="w3_raw", align_bytes=64)
        nc.sync.dma_start(w3_raw[:].bitcast(I32), w3_words[0].bitcast(I32))
        load_scale_rows(xs_raw, x_scales, nc.sync)
        xw_raw = keep.tile([P, T], U32, name="xw_raw", tag="slot0", align_bytes=64)
        nc.sync.dma_start(xw_raw[:].bitcast(I32), x_words[0].rearrange("p n t -> p (n t)").bitcast(I32))
        load_scale_rows(w1s_raw, w1_scales, nc.sync)
        w2_raw = keep.tile([P, 2 * H], U8, name="w2_raw", align_bytes=64)
        nc.sync.dma_start(w2_raw[:].bitcast(I32), w2_words[0].bitcast(I32))
        gm_t = keep.tile([P, PACK], F32, name="gm_t", tag="after_gm", align_bytes=64)
        nc.sync.dma_start(gm_t[:], gm.rearrange("(p t) o -> p (t o)", t=PACK))
        n4_t = load_list(n4, "n4_t")
        n3_t = load_list(n3, "n3_t")
        gn_t = keep.tile([P, PACK], F32, name="gn_t")
        nc.sync.dma_start(gn_t[:], gn.rearrange("(p t) o -> p (t o)", t=PACK))
        n2_t = load_list(n2, "n2_t")
        n1_t = load_list(n1, "n1_t")

        load_scale_rows(w23s_raw, w2_scales, nc.sync)
        load_scale_rows(w23s_raw, w3_scales, nc.sync, 4)
        n5_t = load_list(n5, "n5_t")
        n6_t = load_list(n6, "n6_t")

        w1 = deal_words(w1_raw, "w1")
        w3 = deal_words(w3_raw, "w3")
        xs = keep.tile([P, S], U8, name="xs", align_bytes=64)
        nc.vector.tensor_copy(xs[:], xs_raw[:].indirect(offs_t[:]))
        xw = keep.tile([P, S], U32, name="xw", align_bytes=64)
        nc.vector.tensor_copy(xw[:], xw_raw[:].indirect(offs_t[:]))
        w1s_first = keep.tile([P, P], U8, name="w1s_first", align_bytes=64)
        nc.vector.tensor_copy(w1s_first[:], w1s_raw[:, 0:H:PACK])
        w1s_rest = keep.tile([P, H - P], U8, name="w1s_rest", align_bytes=64)
        nc.vector.tensor_copy(
            w1s_rest[:].rearrange("p (t c i) -> p c t i", t=PACK - 1, i=16),
            w1s_raw[:].rearrange("p (c i t) -> p c t i", t=PACK, i=16)[:, :, 1:, :],
        )

        pg = []
        mem_rows = mem.rearrange("(p t) w -> p t w", t=PACK)
        for t in range(PACK):
            page = keep.tile([P, U], F32, name="pg%d" % t, tag="slot%d" % t, align_bytes=64)
            nc.sync.dma_start(page[:], mem_rows[:, t, :])
            pg.append(page)

        y_ps = [psum.tile([P, S], F32, name="y_ps%d" % t) for t in range(PACK)]
        for t in range(PACK):
            nc.tensor.matmul_mx(
                y_ps[t][:],
                lhsT=w1[:, 2 * P * t : 2 * P * (t + 1)].bitcast(FP4X4),
                lhsT_scale=w1s_rest[:, P * (t - 1) : P * t] if t else w1s_first[:],
                rhs=xw[:].bitcast(FP8X4),
                rhs_scale=xs[:],
                start=True,
                stop=True,
            )

        ya = [keep.tile([P, 2 * S], F32, name="ya%d" % t) for t in range(PACK)]
        ya2 = [keep.tile([P, S], F32, name="yb%d" % t) for t in range(PACK)]
        yn = [keep.tile([P, S], F32, name="yn%d" % t) for t in range(PACK)]
        for t in range(PACK):
            nc.scalar.activation(ym[t][:, :S], y_ps[t][:], ACT.Copy, scale=gm_t[:, t : t + 1])
        for t in range(PACK):
            nc.scalar.activation(ya[t][:, :S], y_ps[t][:], ACT.Abs)
            nc.scalar.activation(ya2[t][:], y_ps[t][:], ACT.Abs)
        for t in range(PACK):
            nc.scalar.activation(yn[t][:], y_ps[t][:], ACT.Copy, scale=gn_t[:, t : t + 1])

        w2 = deal_words(w2_raw, "w2")
        w2s = deal_scales(w23s_raw[:], "w2s")
        for q in range(4):
            nc.sync.dma_start(w3s[32 * q : 32 * q + 4, :].bitcast(I32), w2s[32 * q + 4 : 32 * q + 8, :].bitcast(I32))

        halves = [slice(0, HALF), slice(HALF, S)]
        list_halves = [slice(0, HALF // 16), slice(HALF // 16, S // 16)]

        def tile(shape, dtype, name, tag=None):
            return keep.tile(shape, dtype, name=name, tag=tag or name, align_bytes=64)

        def pair_sum(dst, a, t):
            nc.vector.tensor_tensor(
                dst[:, t, :], ym[t][:].indirect(n3_t[:, list_halves[a]]), ya[t][:, S + a * HALF : S + (a + 1) * HALF], ALU.add
            )

        def invert(t, a, tag=None):
            root = tile([P, HALF], F32, "root%d_%d" % (a, t))
            nc.scalar.activation(root[:], den[t][:, halves[a]], ACT.Abs_reciprocal_sqrt, bias=0.5)
            inv = tile([P, HALF], F32, "inv%d_%d" % (a, t), tag)
            nc.scalar.activation(inv[:], root[:], ACT.Square)
            return inv

        def numerator(dst, a, t, inv):
            nc.vector.tensor_tensor(dst[:, t, :], yn[t][:].indirect(n1_t[:, list_halves[a]]), inv[:], ALU.mult)

        def round_values(values, name, tag=None):
            rounded = tile([P, PACK * HALF], BF16, name, tag)
            interleave(nc.scalar.copy, rounded, values[:])
            return rounded

        def quantise(rounded, name):
            codes = tile([P, HALF], U32, name + "_codes")
            scales = tile([P, HALF], U8, name + "_scales")
            nc.vector.quantize_mx(codes[:].bitcast(FP8X4), scales[:], rounded[:])
            return codes, scales

        h_ps = [psum.tile([P, S], F32, name="h_ps%d" % t) for t in range(PACK)]

        def second_product(a, z2q, zq):
            for t in range(PACK):
                for c in range(0, HALF, PASS_N):
                    cols = slice(c, c + PASS_N)
                    dst = h_ps[t][:, a * HALF + c : a * HALF + c + PASS_N]
                    for first, w, ws, (codes, scales) in ((True, w3, w3s, z2q), (False, w2, w2s, zq)):
                        nc.tensor.matmul_mx(
                            dst,
                            lhsT=w[:, 2 * P * t : 2 * P * (t + 1)].bitcast(FP4X4),
                            lhsT_scale=ws[:, P * t : P * (t + 1)],
                            rhs=codes[:, cols].bitcast(FP8X4),
                            rhs_scale=scales[:, cols],
                            start=first,
                            stop=not first,
                        )

        def fetch_h(h, a, t, scale=1.0):
            nc.scalar.activation(h, h_ps[t][:, halves[a]], ACT.Copy, scale=scale)
            return h

        def scatter(a, t, h):
            nc.vector.tensor_copy(pg[t][:].indirect(n5_t[:, list_halves[a]]), h)

        z2f_a = tile([P, PACK, HALF], F32, "z2f_a", "after_gm")
        for t in range(PACK):
            nc.vector.tensor_scalar(ya[t][:, S:], ym[t][:].indirect(n4_t[:]), 0.75, 0.0, ALU.mult, ALU.add)
        for t in range(PACK):
            pair_sum(z2f_a, 0, t)

        den = [tile([P, S], F32, "den%d" % t) for t in range(PACK)]
        inv_a = []
        for t in range(PACK):
            nc.vector.tensor_tensor(den[t][:], ya[t][:].indirect(n2_t[:]), ya2[t][:], ALU.add)
            inv_a.append(invert(t, 0, "after_zf_a" if t == PACK - 1 else None))
            if t == 0:
                z2b_a = round_values(z2f_a, "z2b_a")
        z2q_a = quantise(z2b_a, "z2q_a")
        zf_a = tile([P, PACK, HALF], F32, "zf_a")
        for t in range(PACK):
            numerator(zf_a, 0, t, inv_a[t])
        inv_b = [invert(t, 1) for t in range(PACK)]
        zb_a = round_values(zf_a, "zb_a", "chain")
        z2f_b = tile([P, PACK, HALF], F32, "z2f_b", "after_zf_a")
        for t in range(PACK):
            pair_sum(z2f_b, 1, t)
        z2b_b = round_values(z2f_b, "z2b_b")
        zq_a = quantise(zb_a, "zq_a")
        zf_b = tile([P, PACK, HALF], F32, "zf_b", "chain")
        for t in range(PACK):
            numerator(zf_b, 1, t, inv_b[t])
        z2q_b = quantise(z2b_b, "z2q_b")
        second_product(0, z2q_a, zq_a)
        for t in range(2):
            scatter(0, t, fetch_h(tile([P, HALF], F32, "h_a%d" % t)[:], 0, t, one[:]))
        zb_b = round_values(zf_b, "zb_b", "after_zq_b")
        zq_b = quantise(zb_b, "zq_b")
        h_late = tile([P, 2, HALF], F32, "h_late", "chain")
        for t in range(2, PACK):
            scatter(0, t, fetch_h(h_late[:, t - 2, :], 0, t))
        second_product(1, z2q_b, zq_b)
        h_b = [fetch_h(tile([P, HALF], F32, "h_b%d" % t)[:], 1, t, one_b[:]) for t in range(PACK)]
        minus_half = tile([P, 1], F32, "minus_half", "after_neg_half")
        nc.scalar.activation(minus_half[:], one_c[:], ACT.Copy, scale=-0.5)
        neg_half = [keep.tile([P, U], F32, name="nh%d" % t) for t in range(PACK)]
        for t in range(PACK):
            scatter(1, t, h_b[t])
            nc.scalar.activation(neg_half[t][:], pg[t][:], ACT.Copy, scale=minus_half[:])

        out_rows = out_0.rearrange("(p t) w -> p t w", t=PACK)
        words_out = out_1[0].rearrange("p n t -> p (n t)").bitcast(I32)
        out_scales = keep.tile([P, U], U8, name="out_scales", align_bytes=64)

        def quantise_out(k, rounded):
            cols = slice(k * OUT_CHUNK, (k + 1) * OUT_CHUNK)
            codes = tile([P, OUT_CHUNK], U32, "codes%d" % k)
            nc.vector.quantize_mx(codes[:].bitcast(FP8X4), out_scales[:, cols], rounded[:])
            nc.sync.dma_start(words_out[:, cols], codes[:].bitcast(I32))

        chunks = U // OUT_CHUNK
        rounded = []
        for k in range(chunks):
            cols = slice(k * OUT_CHUNK, (k + 1) * OUT_CHUNK)
            if k >= 2:
                quantise_out(k - 2, rounded[k - 2])
            res = tile([P, PACK, OUT_CHUNK], F32, "res%d" % k, "out_chain%d" % (k - 2) if k >= 2 else ("after_neg_half" if k else None))
            for t in range(PACK):
                nc.vector.tensor_tensor(
                    res[:, t, :], neg_half[t][:].indirect(n6_t[:, cols.start // 16 : cols.stop // 16]), pg[t][:, cols], ALU.add
                )
                if t % 2 == 1:
                    nc.sync.dma_start(out_rows[:, t - 1 : t + 1, cols], res[:, t - 1 : t + 1, :])
            rounded.append(tile([P, PACK * OUT_CHUNK], BF16, "rounded%d" % k, "out_chain%d" % k if k < 2 else None))
            if k < chunks - 1:
                interleave(nc.scalar.copy, rounded[k], res[:])
            else:
                interleave(nc.vector.tensor_copy, rounded[k][:, : PACK * LAST_SPLIT], res[:, :, :LAST_SPLIT])
                interleave(nc.scalar.copy, rounded[k][:, PACK * LAST_SPLIT :], res[:, :, LAST_SPLIT:])
        quantise_out(chunks - 2, rounded[chunks - 2])
        quantise_out(chunks - 1, rounded[chunks - 1])
        for q in range(4):
            queue = nc.sync if q % 2 == 0 else nc.scalar
            queue.dma_start(out_2[0, 4 * q : 4 * q + 4, :].bitcast(I32), out_scales[32 * q : 32 * q + 4, :].bitcast(I32))
